import numpy as np
import ml_dtypes


def mxq(x, axis, fmt="e4m3"):
    dtype, down = {"e4m3": (ml_dtypes.float8_e4m3fn, 7), "e5m2": (ml_dtypes.float8_e5m2, 14)}[fmt]
    v = np.moveaxis(np.asarray(x, np.float32).astype(ml_dtypes.bfloat16).astype(np.float64), axis, -1)
    blocks = v.reshape(v.shape[:-1] + (-1, 32))
    amax = np.abs(blocks).max(-1, keepdims=True)
    byte = np.maximum(np.where(amax > 0, np.frexp(amax)[1] - 1 + 127, 0) - down, 1)
    scale = np.exp2(byte - 127.0)
    codes = (blocks / scale).astype(np.float32).astype(dtype).astype(np.float64)
    return np.moveaxis((codes * scale).reshape(v.shape), -1, axis)


WIDE = False


def mx_kscale(k):
    if not WIDE:
        return np.ones(k)
    levels = np.array([10, -10, 5, -5, 0])
    if k % 512:
        return np.exp2(np.random.permutation(np.resize(levels, k // 32))).repeat(32)
    a = np.empty((k // 512, 16))
    for p in range(k // 512):
        a[p, :8] = np.random.permutation(np.resize(levels, 8))
        for g in range(8):
            far = levels[np.abs(levels - a[p, g]) >= 10]
            a[p, g + 8] = far[np.random.randint(len(far))]
    return np.exp2(a.ravel()).repeat(32)


def f64(x):
    return np.asarray(x).astype(np.float64)


def striped(idx):
    return np.tile(np.asarray(idx).reshape(-1, 16).T, (8, 1)).astype(np.uint16)


def unstriped(offs):
    return offs[:16].T.reshape(-1).astype(np.int64)


E2M1 = np.array([0.0, 0.5, 1.0, 1.5, 2.0, 3.0, 4.0, 6.0, -0.0, -0.5, -1.0, -1.5, -2.0, -3.0, -4.0, -6.0])


def pack_weight(w, fmt):
    k, n = w.shape
    w = f64(np.asarray(w, np.float32).astype(ml_dtypes.bfloat16)).reshape(k // 32, 32, n)
    amax = np.abs(w).max(1)
    if fmt == "e4m3":
        byte = np.frexp(amax)[1] - 1 + 127 - 7
    else:
        mant, ex = np.frexp(amax / 6.0)
        byte = np.where(mant > 0.5, ex, ex - 1) + 127
    byte = np.clip(np.where(amax > 0, byte, 1), 1, 254)
    scaled = (w * np.exp2(127.0 - byte)[:, None, :]).reshape(k, n).astype(np.float32)
    by_word = np.ascontiguousarray(scaled.reshape(k // 512, 128, 4, n).transpose(0, 1, 3, 2))
    if fmt == "e4m3":
        words = by_word.astype(ml_dtypes.float8_e4m3fn).view(np.uint8)
    else:
        c = by_word.astype(ml_dtypes.float4_e2m1fn).view(np.uint8) & 0xF
        words = (c[..., 0::2] | (c[..., 1::2] << 4)).reshape(k // 512, 128, 2 * n)
    return np.ascontiguousarray(words), np.ascontiguousarray(byte.astype(np.uint8).reshape(k // 512, 16, n))


def unpack_weight(words, scales, fmt):
    g, _, n = scales.shape
    words = np.ascontiguousarray(words).reshape(g, 128, n, -1)
    if fmt == "e4m3":
        vals = words.view(ml_dtypes.float8_e4m3fn).astype(np.float64)
    else:
        nib = np.empty((g, 128, n, 4), np.uint8)
        nib[..., 0::2] = words & 0xF
        nib[..., 1::2] = words >> 4
        vals = E2M1[nib]
    vals = vals * np.repeat(np.exp2(scales.astype(np.float64) - 127.0), 8, axis=1)[..., None]
    return vals.transpose(0, 1, 3, 2).reshape(g * 512, n)


def bf(x):
    return np.asarray(x, np.float32).astype(ml_dtypes.bfloat16)


def planes(Y):
    r, m = Y.shape
    b = f64(bf(Y)).reshape(r // 32, 32, m)
    amax = np.abs(b).max(1)
    byte = np.clip(np.where(amax > 0, np.frexp(amax)[1] - 1 + 127 - 7, 1), 1, 254)
    codes = (b * np.exp2(127.0 - byte)[:, None, :]).reshape(r, m).astype(np.float32).astype(ml_dtypes.float8_e4m3fn).view(np.uint8)
    words = codes.reshape(r // 512, 128, 4, m).transpose(0, 1, 3, 2)
    return np.ascontiguousarray(words), np.ascontiguousarray(byte.astype(np.uint8).reshape(r // 512, 16, m))


D, T, I, J, U, Z, M = 512, 2048, 512, 512, 1024, 1024, 1024


def setup_inputs():
    n = np.random.standard_normal
    idx = np.random.permutation(T)[:I]
    idx2 = np.random.permutation(U)[:J]
    idx3 = np.random.permutation(Z)[:J]
    idx4 = np.random.permutation(M)[:J]
    fd = mx_kscale(D)
    keysp = pack_weight(n((D, T)) / fd[:, None], "e2m1")
    return {
        "keys_words": keysp[0],
        "keys_scales": keysp[1],
        "notes": (n((D, U)) * 1.0 / np.sqrt(D) * fd[:, None]).astype(np.float32),
        "users2": (n((D, Z)) * 1.0 / np.sqrt(D) * fd[:, None]).astype(np.float32),
        "old": (1.0 * n((I, M))).astype(np.float32),
        "fade": (np.random.uniform(0.3, 0.9, (I, 1))).astype(np.float32),
        "offs": striped(idx),
        "offs2": striped(idx2),
        "offs3": striped(idx3),
        "offs4": striped(idx4),
    }


def reference(keys_words, keys_scales, notes, users2, old, fade, offs, offs2, offs3, offs4):
    idx = unstriped(offs)
    idx2 = unstriped(offs2)
    idx3 = unstriped(offs3)
    idx4 = unstriped(offs4)
    keysu = unpack_weight(keys_words, keys_scales, "e2m1")
    keysidxg = keysu[:, idx]
    notesidx2q = mxq(f64(notes)[:, idx2], 0, "e4m3")
    g1 = keysidxg.T @ notesidx2q
    users2idx3q = mxq(f64(users2)[:, idx3], 0, "e4m3")
    g2 = keysidxg.T @ users2idx3q
    g0 = np.maximum(g1, g2)
    gf = np.zeros((I, M))
    gf[:, idx4] = g0
    y = f64(old) * f64(fade) + gf
    words, scales = planes(y)
    return y, words, scales

@@ -1,0 +1,212 @@
+from contextlib import ExitStack
+
+import concourse.mybir as mybir
+
+D, T, I, J, U, M = 512, 2048, 512, 512, 1024, 1024
+FLOPS = 2 * 2 * D * I * J
+
+F32 = mybir.dt.float32
+BF16 = mybir.dt.bfloat16
+I32 = mybir.dt.int32
+U32 = mybir.dt.uint32
+U16 = mybir.dt.uint16
+U8 = mybir.dt.uint8
+FP8X4 = mybir.dt.float8_e4m3fn_x4
+FP4X4 = mybir.dt.float4_e2m1fn_x4
+COPY = mybir.ActivationFunctionType.Copy
+ALU = mybir.AluOpType
+
+P = 128
+PACK = 4
+HALF = J // 2
+LIST_COLS = J // 16
+
+
+def tile_attend_tab_larger_keep_pl_kernel(
+    tc, keys_words, keys_scales, notes, users2, old, fade, offs, offs2, offs3, offs4, out_0, out_1, out_2
+):
+    nc = tc.nc
+    with ExitStack() as ctx:
+        sb = ctx.enter_context(tc.tile_pool(name="sb", bufs=1))
+        ps = ctx.enter_context(tc.psum_pool(name="ps", bufs=1))
+
+        def tiles(name, count, shape, dtype):
+            return [sb.tile(shape, dtype, name="%s%d" % (name, n), align_bytes=64) for n in range(count)]
+
+        key_list = sb.tile([P, LIST_COLS], U16, name="key_list")
+        note_list = sb.tile([P, LIST_COLS], U16, name="note_list")
+        user_list = sb.tile([P, LIST_COLS], U16, name="user_list")
+        place_list = sb.tile([P, LIST_COLS], U16, name="place_list")
+        key_word_pool = sb.tile([P, T], U16, name="key_word_pool", align_bytes=64)
+        key_scale_pool = sb.tile([P, T], U8, name="key_scale_pool", align_bytes=64)
+        note_rows = tiles("note_rows", PACK, [P, U], F32)
+        user_rows = tiles("user_rows", PACK - 1, [P, U], F32)
+        user_rows.append(sb.tile([P, U], F32, name="user_rows_last", tag="last_users_then_g1", align_bytes=64))
+        old_rows = tiles("old_rows", PACK, [P, M], F32)
+        placed = tiles("placed", PACK, [P, M], F32)
+        fade_cols = sb.tile([P, PACK], F32, name="fade_cols")
+
+        notes_by_slot = notes.rearrange("(p t) u -> t p u", t=PACK)
+        users_by_slot = users2.rearrange("(p t) u -> t p u", t=PACK)
+        old_by_slot = old.rearrange("(p r) m -> r p m", r=PACK)
+        out_by_slot = out_0.rearrange("(p r) m -> r p m", r=PACK)
+
+        nc.vector.memset(key_scale_pool[:].bitcast(I32), 0)
+        for r in range(PACK):
+            nc.vector.memset(placed[r][:], 0.0)
+
+        nc.sync.dma_start(note_list[:], offs2)
+        nc.sync.dma_start(note_rows[0][:], notes_by_slot[0])
+        for q in range(4):
+            nc.sync.dma_start(
+                key_scale_pool[32 * q : 32 * q + 4, :].bitcast(I32),
+                keys_scales[0, 4 * q : 4 * q + 4, :].bitcast(I32),
+            )
+        nc.sync.dma_start(note_rows[1][:], notes_by_slot[1])
+        nc.sync.dma_start(key_list[:], offs)
+        nc.sync.dma_start(key_word_pool[:].bitcast(I32), keys_words[0].bitcast(I32))
+        nc.sync.dma_start(note_rows[2][:], notes_by_slot[2])
+        nc.sync.dma_start(note_rows[3][:], notes_by_slot[3])
+        nc.sync.dma_start(user_list[:], offs3)
+        for t in range(PACK):
+            nc.sync.dma_start(user_rows[t][:], users_by_slot[t])
+        nc.sync.dma_start(place_list[:], offs4)
+        nc.sync.dma_start(fade_cols[:], fade.rearrange("(p r) o -> p (r o)", r=PACK))
+        for r in (0, 2, 1, 3):
+            nc.sync.dma_start(old_rows[r][:], old_by_slot[r])
+
+        def half_list(lst, h):
+            return lst[:, h * (HALF // 16) : (h + 1) * (HALF // 16)]
+
+        def half_cols(h):
+            return slice(h * HALF, (h + 1) * HALF)
+
+        picked_words = sb.tile([P, I], U16, name="picked_words", align_bytes=64)
+        key_words = sb.tile([P, PACK, P], U16, name="key_words", align_bytes=64)
+        key_scales = sb.tile([P, PACK, P], U8, name="key_scales", align_bytes=64)
+        nc.vector.tensor_copy(picked_words[:], key_word_pool[:].indirect(key_list[:]))
+        nc.vector.tensor_copy(
+            key_scales[:].rearrange("p r s -> p s r"), key_scale_pool[:].indirect(key_list[:])
+        )
+        nc.vector.tensor_copy(key_words[:], picked_words[:].rearrange("p (s r) -> p r s", r=PACK))
+
+        def weave(dst, src, width):
+            nc.vector.tensor_copy(
+                dst.rearrange("p (c i) t -> p c t i", i=4), src.rearrange("p t (c i) -> p c t i", i=4)
+            )
+
+        picked_notes = sb.tile([P, PACK, J], BF16, name="picked_notes", align_bytes=64)
+        for t in range(PACK):
+            if t in (0, PACK - 1):
+                nc.vector.tensor_copy(picked_notes[:, t, half_cols(0)], note_rows[t][:].indirect(half_list(note_list, 0)))
+                nc.scalar.activation(picked_notes[:, t, half_cols(1)], note_rows[t][:].indirect(half_list(note_list, 1)), COPY)
+            else:
+                nc.scalar.activation(picked_notes[:, t, :], note_rows[t][:].indirect(note_list[:]), COPY)
+        woven_notes = sb.tile([P, J, PACK], BF16, name="woven_notes", align_bytes=64)
+        note_codes = sb.tile([P, J], U32, name="note_codes", align_bytes=64)
+        note_scales = sb.tile([P, J], U8, name="note_scales", align_bytes=64)
+        weave(woven_notes[:], picked_notes[:], J)
+        nc.vector.quantize_mx(
+            note_codes[:].bitcast(FP8X4), note_scales[:], woven_notes[:].rearrange("p j t -> p (j t)")
+        )
+        g1_banks = [ps.tile([P, J], F32, name="g1_bank%d" % r) for r in range(PACK)]
+        for r in (2, 1, 0, 3):
+            nc.tensor.matmul_mx(
+                g1_banks[r][:], key_words[:, r, :].bitcast(FP4X4), key_scales[:, r, :],
+                note_codes[:].bitcast(FP8X4), note_scales[:], start=True, stop=True,
+            )
+
+        picked_users = tiles("picked_users", 2, [P, PACK, HALF], BF16)
+        woven_users = tiles("woven_users", 2, [P, HALF, PACK], BF16)
+        user_codes = tiles("user_codes", 2, [P, HALF], U32)
+        user_scales = tiles("user_scales", 2, [P, HALF], U8)
+        g0_first = tiles("g0_first", 2, [P, 2, HALF], F32)
+        y = sb.tile([P, PACK, M], F32, name="y", align_bytes=64)
+        ORDER = (2, 1, 0, 3)
+        y_flat = y[:].rearrange("p r m -> p (r m)")
+        y_blocks = y_flat.rearrange("p (b x) -> p b x", x=HALF)
+
+        for t in range(PACK):
+            for h in range(2):
+                src = user_rows[t][:].indirect(half_list(user_list, h))
+                if t >= 2 and h == 0:
+                    nc.vector.tensor_copy(picked_users[h][:, t, :], src)
+                else:
+                    nc.scalar.activation(picked_users[h][:, t, :], src, COPY)
+        g1 = sb.tile([P, PACK, J], F32, name="g1", tag="last_users_then_g1", align_bytes=64)
+        for n in range(PACK):
+            nc.scalar.copy(g1[:, n, :], g1_banks[ORDER[n]][:])
+        for h in range(2):
+            weave(woven_users[h][:], picked_users[h][:], HALF)
+            nc.vector.quantize_mx(
+                user_codes[h][:].bitcast(FP8X4), user_scales[h][:], woven_users[h][:].rearrange("p j t -> p (j t)")
+            )
+        for h in range(2):
+            for pair in range(2):
+                bank = ps.tile([P, 2, HALF], F32, name="g2_bank%d%d" % (h, pair))
+                for e in range(2):
+                    r = ORDER[2 * pair + e]
+                    nc.tensor.matmul_mx(
+                        bank[:, e, :], key_words[:, r, :].bitcast(FP4X4), key_scales[:, r, :],
+                        user_codes[h][:].bitcast(FP8X4), user_scales[h][:], start=True, stop=True,
+                    )
+                nc.vector.tensor_tensor(
+                    g0_first[h][:] if pair == 0 else y_blocks[:, 7 + h : 13 + h : 5, :], bank[:],
+                    g1[:, 2 * pair : 2 * pair + 2, h * HALF : (h + 1) * HALF], ALU.max,
+                )
+
+        woven_y = sb.tile([P, M, PACK], BF16, name="woven_y", align_bytes=64)
+        y_codes = sb.tile([P, M], U32, name="y_codes", align_bytes=64)
+        y_scales = sb.tile([P, M], U8, name="y_scales", align_bytes=64)
+
+        def scatter(r, first, last, src, on_vector):
+            dst = placed[r][:].indirect(place_list[:, first // 16 : last // 16])
+            if on_vector:
+                nc.vector.tensor_copy(dst, src)
+            else:
+                nc.scalar.activation(dst, src, COPY)
+
+        def add_old(r, cols):
+            nc.vector.scalar_tensor_tensor(
+                y[:, r, cols], old_rows[r][:, cols], fade_cols[:, r : r + 1], placed[r][:, cols], ALU.mult, ALU.add
+            )
+
+        def round_rows(cols, on_vector):
+            dst = woven_y[:, cols, :].rearrange("p (c i) r -> p c r i", i=4)
+            src = y[:, :, cols].rearrange("p r (c i) -> p c r i", i=4)
+            if on_vector:
+                nc.vector.tensor_copy(dst, src)
+            else:
+                nc.scalar.copy(dst, src)
+
+        everything = slice(0, M)
+        quarters = [slice(c * M // 4, (c + 1) * M // 4) for c in range(4)]
+        halves = [slice(0, M // 2), slice(M // 2, M)]
+        split = 128
+        scatter(3, 0, split, y[:, 3, 0:split], True)
+        scatter(0, 0, J, y_flat[:, 7 * HALF : 9 * HALF], True)
+        for n in range(2):
+            for h in range(2):
+                scatter(ORDER[n], h * HALF, (h + 1) * HALF, g0_first[h][:, n, :], False)
+        scatter(3, split, J, y[:, 3, split:J], False)
+        for r in (0, 2, 1):
+            add_old(r, everything)
+            nc.sync.dma_start(out_by_slot[r], y[:, r, :])
+        words_out = out_1[0].rearrange("p c r -> p (c r)").bitcast(I32)
+        for c in range(4):
+            add_old(PACK - 1, quarters[c])
+        for c in range(2):
+            nc.sync.dma_start(out_by_slot[PACK - 1][:, halves[c]], y[:, PACK - 1, halves[c]])
+        for c in range(4):
+            round_rows(quarters[c], c >= 2)
+        for c in (1, 0):
+            nc.vector.quantize_mx(
+                y_codes[:, halves[c]].bitcast(FP8X4), y_scales[:, halves[c]],
+                woven_y[:, halves[c], :].rearrange("p m r -> p (m r)"),
+            )
+            nc.sync.dma_start(words_out[:, halves[c]], y_codes[:, halves[c]].bitcast(I32))
+        for q in range(4):
+            queue = nc.sync if q % 2 == 0 else nc.scalar
+            queue.dma_start(
+                out_2[0, 4 * q : 4 * q + 4, :].bitcast(I32), y_scales[32 * q : 32 * q + 4, :].bitcast(I32)
+            )

@@ -52,25 +52,26 @@ def tile_attend_tab_larger_keep_pl_kernel(
         out_by_slot = out_0.rearrange("(p r) m -> r p m", r=PACK)
 
         nc.vector.memset(key_scale_pool[:].bitcast(I32), 0)
-        for r in range(PACK):
-            nc.vector.memset(placed[r][:], 0.0)
+        nc.vector.memset(placed[0][:], 0.0)
+        for r in range(1, PACK):
+            nc.gpsimd.memset(placed[r][:], 0.0)
 
-        nc.sync.dma_start(note_list[:], offs2)
         nc.sync.dma_start(note_rows[0][:], notes_by_slot[0])
+        nc.sync.dma_start(note_list[:], offs2)
+        nc.sync.dma_start(key_list[:], offs)
+        nc.sync.dma_start(key_word_pool[:].bitcast(I32), keys_words[0].bitcast(I32))
+        nc.sync.dma_start(user_list[:], offs3)
+        nc.sync.dma_start(place_list[:], offs4)
+        nc.sync.dma_start(note_rows[1][:], notes_by_slot[1])
+        nc.sync.dma_start(note_rows[2][:], notes_by_slot[2])
         for q in range(4):
             nc.sync.dma_start(
                 key_scale_pool[32 * q : 32 * q + 4, :].bitcast(I32),
                 keys_scales[0, 4 * q : 4 * q + 4, :].bitcast(I32),
             )
-        nc.sync.dma_start(note_rows[1][:], notes_by_slot[1])
-        nc.sync.dma_start(key_list[:], offs)
-        nc.sync.dma_start(key_word_pool[:].bitcast(I32), keys_words[0].bitcast(I32))
-        nc.sync.dma_start(note_rows[2][:], notes_by_slot[2])
         nc.sync.dma_start(note_rows[3][:], notes_by_slot[3])
-        nc.sync.dma_start(user_list[:], offs3)
         for t in range(PACK):
             nc.sync.dma_start(user_rows[t][:], users_by_slot[t])
-        nc.sync.dma_start(place_list[:], offs4)
         nc.sync.dma_start(fade_cols[:], fade.rearrange("(p r) o -> p (r o)", r=PACK))
         for r in (0, 2, 1, 3):
             nc.sync.dma_start(old_rows[r][:], old_by_slot[r])
@@ -117,7 +118,6 @@ def tile_attend_tab_larger_keep_pl_kernel(
             )
 
         picked_users = tiles("picked_users", 2, [P, PACK, HALF], BF16)
-        woven_users = tiles("woven_users", 2, [P, HALF, PACK], BF16)
         user_codes = tiles("user_codes", 2, [P, HALF], U32)
         user_scales = tiles("user_scales", 2, [P, HALF], U8)
         g0_first = tiles("g0_first", 2, [P, 2, HALF], F32)
@@ -137,11 +137,11 @@ def tile_attend_tab_larger_keep_pl_kernel(
         for n in range(PACK):
             nc.scalar.copy(g1[:, n, :], g1_banks[ORDER[n]][:])
         for h in range(2):
-            weave(woven_users[h][:], picked_users[h][:], HALF)
+            woven_users = sb.tile([P, HALF, PACK], BF16, name="woven_users", align_bytes=64)
+            weave(woven_users[:], picked_users[h][:], HALF)
             nc.vector.quantize_mx(
-                user_codes[h][:].bitcast(FP8X4), user_scales[h][:], woven_users[h][:].rearrange("p j t -> p (j t)")
+                user_codes[h][:].bitcast(FP8X4), user_scales[h][:], woven_users[:].rearrange("p j t -> p (j t)")
             )
-        for h in range(2):
             for pair in range(2):
                 bank = ps.tile([P, 2, HALF], F32, name="g2_bank%d%d" % (h, pair))
                 for e in range(2):
@@ -182,23 +182,23 @@ def tile_attend_tab_larger_keep_pl_kernel(
         everything = slice(0, M)
         quarters = [slice(c * M // 4, (c + 1) * M // 4) for c in range(4)]
         halves = [slice(0, M // 2), slice(M // 2, M)]
-        split = 128
-        scatter(3, 0, split, y[:, 3, 0:split], True)
+        split = J - 128
+        scatter(3, split, J, y[:, 3, split:J], True)
         scatter(0, 0, J, y_flat[:, 7 * HALF : 9 * HALF], True)
         for n in range(2):
             for h in range(2):
                 scatter(ORDER[n], h * HALF, (h + 1) * HALF, g0_first[h][:, n, :], False)
-        scatter(3, split, J, y[:, 3, split:J], False)
+        scatter(3, 0, split, y[:, 3, 0:split], False)
         for r in (0, 2, 1):
             add_old(r, everything)
             nc.sync.dma_start(out_by_slot[r], y[:, r, :])
         words_out = out_1[0].rearrange("p c r -> p (c r)").bitcast(I32)
-        for c in range(4):
-            add_old(PACK - 1, quarters[c])
+        add_old(PACK - 1, quarters[0])
+        add_old(PACK - 1, slice(M // 4, M))
+        nc.sync.dma_start(out_by_slot[PACK - 1], y[:, PACK - 1, :])
         for c in range(2):
-            nc.sync.dma_start(out_by_slot[PACK - 1][:, halves[c]], y[:, PACK - 1, halves[c]])
-        for c in range(4):
-            round_rows(quarters[c], c >= 2)
+            round_rows(quarters[c], False)
+        round_rows(halves[1], True)
         for c in (1, 0):
             nc.vector.quantize_mx(
                 y_codes[:, halves[c]].bitcast(FP8X4), y_scales[:, halves[c]],

@@ -18,8 +18,16 @@ ALU = mybir.AluOpType
 
 P = 128
 PACK = 4
+QUADRANTS = 4
+PER_COLUMN = 16
+RUN = 4
 HALF = J // 2
-LIST_COLS = J // 16
+
+FIRST, SECOND, OWN, LAST = 0, 1, 2, 3
+PAIRS = ((LAST, FIRST), (SECOND, OWN))
+BY_PAIR = PAIRS[0] + PAIRS[1]
+LAST_ON_VECTOR = 256
+WOVEN_ON_SCALAR = 128
 
 
 def tile_attend_tab_larger_keep_pl_kernel(
@@ -33,134 +41,143 @@ def tile_attend_tab_larger_keep_pl_kernel(
         def tiles(name, count, shape, dtype):
             return [sb.tile(shape, dtype, name="%s%d" % (name, n), align_bytes=64) for n in range(count)]
 
-        key_list = sb.tile([P, LIST_COLS], U16, name="key_list")
-        note_list = sb.tile([P, LIST_COLS], U16, name="note_list")
-        user_list = sb.tile([P, LIST_COLS], U16, name="user_list")
-        place_list = sb.tile([P, LIST_COLS], U16, name="place_list")
+        def entries(offsets, first, last):
+            return offsets[:, first // PER_COLUMN : last // PER_COLUMN]
+
+        def half_cols(h):
+            return slice(h * HALF, (h + 1) * HALF)
+
+        def gather(dst, slab, offsets, on_vector):
+            if on_vector:
+                nc.vector.tensor_copy(dst, slab[:].indirect(offsets))
+            else:
+                nc.scalar.activation(dst, slab[:].indirect(offsets), COPY)
+
+        def weave(dst, src, on_vector):
+            dst = dst.rearrange("p (c n) t -> p c t n", n=RUN)
+            src = src.rearrange("p t (c n) -> p c t n", n=RUN)
+            if on_vector:
+                nc.vector.tensor_copy(dst, src)
+            else:
+                nc.scalar.copy(dst, src)
+
+        def quantise(codes, scales, woven):
+            nc.vector.quantize_mx(codes.bitcast(FP8X4), scales, woven.rearrange("p c t -> p (c t)"))
+
+        key_list = sb.tile([P, I // PER_COLUMN], U16, name="key_list")
+        note_list = sb.tile([P, J // PER_COLUMN], U16, name="note_list")
+        user_list = sb.tile([P, J // PER_COLUMN], U16, name="user_list")
+        place_list = sb.tile([P, J // PER_COLUMN], U16, name="place_list")
         key_word_pool = sb.tile([P, T], U16, name="key_word_pool", align_bytes=64)
         key_scale_pool = sb.tile([P, T], U8, name="key_scale_pool", align_bytes=64)
-        note_rows = tiles("note_rows", PACK, [P, U], F32)
-        user_rows = tiles("user_rows", PACK - 1, [P, U], F32)
-        user_rows.append(sb.tile([P, U], F32, name="user_rows_last", tag="last_users_then_g1", align_bytes=64))
-        old_rows = tiles("old_rows", PACK, [P, M], F32)
+        note_slabs = tiles("note_slab", PACK, [P, U], F32)
+        user_slabs = tiles("user_slab", PACK - 1, [P, U], F32)
+        user_slabs.append(sb.tile([P, U], F32, name="user_slab_last", tag="last_users_then_g1", align_bytes=64))
+        old_slabs = tiles("old_slab", PACK, [P, M], F32)
         placed = tiles("placed", PACK, [P, M], F32)
         fade_cols = sb.tile([P, PACK], F32, name="fade_cols")
 
-        notes_by_slot = notes.rearrange("(p t) u -> t p u", t=PACK)
-        users_by_slot = users2.rearrange("(p t) u -> t p u", t=PACK)
-        old_by_slot = old.rearrange("(p r) m -> r p m", r=PACK)
-        out_by_slot = out_0.rearrange("(p r) m -> r p m", r=PACK)
+        notes_by_slab = notes.rearrange("(p t) u -> t p u", t=PACK)
+        users_by_slab = users2.rearrange("(p t) u -> t p u", t=PACK)
+        old_by_slab = old.rearrange("(p r) m -> r p m", r=PACK)
+        out_by_slab = out_0.rearrange("(p r) m -> r p m", r=PACK)
 
         nc.vector.memset(key_scale_pool[:].bitcast(I32), 0)
         nc.vector.memset(placed[0][:], 0.0)
         for r in range(1, PACK):
             nc.gpsimd.memset(placed[r][:], 0.0)
 
-        nc.sync.dma_start(note_rows[0][:], notes_by_slot[0])
+        nc.sync.dma_start(note_slabs[0][:], notes_by_slab[0])
         nc.sync.dma_start(note_list[:], offs2)
         nc.sync.dma_start(key_list[:], offs)
         nc.sync.dma_start(key_word_pool[:].bitcast(I32), keys_words[0].bitcast(I32))
         nc.sync.dma_start(user_list[:], offs3)
         nc.sync.dma_start(place_list[:], offs4)
-        nc.sync.dma_start(note_rows[1][:], notes_by_slot[1])
-        nc.sync.dma_start(note_rows[2][:], notes_by_slot[2])
-        for q in range(4):
+        nc.sync.dma_start(note_slabs[1][:], notes_by_slab[1])
+        nc.sync.dma_start(note_slabs[2][:], notes_by_slab[2])
+        for q in range(QUADRANTS):
             nc.sync.dma_start(
                 key_scale_pool[32 * q : 32 * q + 4, :].bitcast(I32),
                 keys_scales[0, 4 * q : 4 * q + 4, :].bitcast(I32),
             )
-        nc.sync.dma_start(note_rows[3][:], notes_by_slot[3])
+        nc.sync.dma_start(note_slabs[3][:], notes_by_slab[3])
         for t in range(PACK):
-            nc.sync.dma_start(user_rows[t][:], users_by_slot[t])
+            nc.sync.dma_start(user_slabs[t][:], users_by_slab[t])
         nc.sync.dma_start(fade_cols[:], fade.rearrange("(p r) o -> p (r o)", r=PACK))
-        for r in (0, 2, 1, 3):
-            nc.sync.dma_start(old_rows[r][:], old_by_slot[r])
-
-        def half_list(lst, h):
-            return lst[:, h * (HALF // 16) : (h + 1) * (HALF // 16)]
-
-        def half_cols(h):
-            return slice(h * HALF, (h + 1) * HALF)
+        for r in (FIRST, OWN, SECOND, LAST):
+            nc.sync.dma_start(old_slabs[r][:], old_by_slab[r])
 
         picked_words = sb.tile([P, I], U16, name="picked_words", align_bytes=64)
         key_words = sb.tile([P, PACK, P], U16, name="key_words", align_bytes=64)
         key_scales = sb.tile([P, PACK, P], U8, name="key_scales", align_bytes=64)
         nc.vector.tensor_copy(picked_words[:], key_word_pool[:].indirect(key_list[:]))
-        nc.vector.tensor_copy(
-            key_scales[:].rearrange("p r s -> p s r"), key_scale_pool[:].indirect(key_list[:])
-        )
+        nc.vector.tensor_copy(key_scales[:].rearrange("p r s -> p s r"), key_scale_pool[:].indirect(key_list[:]))
         nc.vector.tensor_copy(key_words[:], picked_words[:].rearrange("p (s r) -> p r s", r=PACK))
 
-        def weave(dst, src, width):
-            nc.vector.tensor_copy(
-                dst.rearrange("p (c i) t -> p c t i", i=4), src.rearrange("p t (c i) -> p c t i", i=4)
+        def product(bank, r, codes, scales):
+            nc.tensor.matmul_mx(
+                bank, key_words[:, r, :].bitcast(FP4X4), key_scales[:, r, :], codes.bitcast(FP8X4), scales,
+                start=True, stop=True,
             )
 
         picked_notes = sb.tile([P, PACK, J], BF16, name="picked_notes", align_bytes=64)
         for t in range(PACK):
             if t in (0, PACK - 1):
-                nc.vector.tensor_copy(picked_notes[:, t, half_cols(0)], note_rows[t][:].indirect(half_list(note_list, 0)))
-                nc.scalar.activation(picked_notes[:, t, half_cols(1)], note_rows[t][:].indirect(half_list(note_list, 1)), COPY)
+                gather(picked_notes[:, t, half_cols(0)], note_slabs[t], entries(note_list, 0, HALF), True)
+                gather(picked_notes[:, t, half_cols(1)], note_slabs[t], entries(note_list, HALF, J), False)
             else:
-                nc.scalar.activation(picked_notes[:, t, :], note_rows[t][:].indirect(note_list[:]), COPY)
+                gather(picked_notes[:, t, :], note_slabs[t], note_list[:], False)
         woven_notes = sb.tile([P, J, PACK], BF16, name="woven_notes", align_bytes=64)
         note_codes = sb.tile([P, J], U32, name="note_codes", align_bytes=64)
         note_scales = sb.tile([P, J], U8, name="note_scales", align_bytes=64)
-        weave(woven_notes[:], picked_notes[:], J)
-        nc.vector.quantize_mx(
-            note_codes[:].bitcast(FP8X4), note_scales[:], woven_notes[:].rearrange("p j t -> p (j t)")
-        )
+        weave(woven_notes[:], picked_notes[:], True)
+        quantise(note_codes[:], note_scales[:], woven_notes[:])
         g1_banks = [ps.tile([P, J], F32, name="g1_bank%d" % r) for r in range(PACK)]
-        for r in (2, 1, 0, 3):
-            nc.tensor.matmul_mx(
-                g1_banks[r][:], key_words[:, r, :].bitcast(FP4X4), key_scales[:, r, :],
-                note_codes[:].bitcast(FP8X4), note_scales[:], start=True, stop=True,
-            )
+        for r in BY_PAIR:
+            product(g1_banks[r][:], r, note_codes[:], note_scales[:])
 
         picked_users = tiles("picked_users", 2, [P, PACK, HALF], BF16)
         user_codes = tiles("user_codes", 2, [P, HALF], U32)
         user_scales = tiles("user_scales", 2, [P, HALF], U8)
-        g0_first = tiles("g0_first", 2, [P, 2, HALF], F32)
         y = sb.tile([P, PACK, M], F32, name="y", align_bytes=64)
-        ORDER = (2, 1, 0, 3)
-        y_flat = y[:].rearrange("p r m -> p (r m)")
-        y_blocks = y_flat.rearrange("p (b x) -> p b x", x=HALF)
-
         for t in range(PACK):
             for h in range(2):
-                src = user_rows[t][:].indirect(half_list(user_list, h))
-                if t >= 2 and h == 0:
-                    nc.vector.tensor_copy(picked_users[h][:, t, :], src)
-                else:
-                    nc.scalar.activation(picked_users[h][:, t, :], src, COPY)
+                offsets = entries(user_list, h * HALF, (h + 1) * HALF)
+                gather(picked_users[h][:, t, :], user_slabs[t], offsets, t >= PACK - 2 and h == 0)
+        woven_users = [
+            sb.tile([P, HALF, PACK], BF16, name="woven_users0", align_bytes=64),
+            sb.tile([P, HALF, PACK], BF16, name="woven_users1", tag="woven_then_faded", align_bytes=64),
+        ]
+        by_scalar = slice(HALF - WOVEN_ON_SCALAR, HALF)
+        weave(woven_users[1][:, by_scalar, :], picked_users[1][:, :, by_scalar], False)
+
         g1 = sb.tile([P, PACK, J], F32, name="g1", tag="last_users_then_g1", align_bytes=64)
         for n in range(PACK):
-            nc.scalar.copy(g1[:, n, :], g1_banks[ORDER[n]][:])
+            nc.scalar.copy(g1[:, n, :], g1_banks[BY_PAIR[n]][:])
+
         for h in range(2):
-            woven_users = sb.tile([P, HALF, PACK], BF16, name="woven_users", align_bytes=64)
-            weave(woven_users[:], picked_users[h][:], HALF)
-            nc.vector.quantize_mx(
-                user_codes[h][:].bitcast(FP8X4), user_scales[h][:], woven_users[:].rearrange("p j t -> p (j t)")
-            )
-            for pair in range(2):
-                bank = ps.tile([P, 2, HALF], F32, name="g2_bank%d%d" % (h, pair))
-                for e in range(2):
-                    r = ORDER[2 * pair + e]
-                    nc.tensor.matmul_mx(
-                        bank[:, e, :], key_words[:, r, :].bitcast(FP4X4), key_scales[:, r, :],
-                        user_codes[h][:].bitcast(FP8X4), user_scales[h][:], start=True, stop=True,
-                    )
+            by_vector = slice(0, HALF if h == 0 else HALF - WOVEN_ON_SCALAR)
+            weave(woven_users[h][:, by_vector, :], picked_users[h][:, :, by_vector], True)
+            quantise(user_codes[h][:], user_scales[h][:], woven_users[h][:])
+
+        for k, pair in enumerate(PAIRS):
+            waiting = y[:, pair[0], :].rearrange("p (e j) -> p e j", e=2)
+            for h in range(2):
+                bank = ps.tile([P, 2, HALF], F32, name="g2_bank%d%d" % (h, k))
+                for e, r in enumerate(pair):
+                    product(bank[:, e, :], r, user_codes[h][:], user_scales[h][:])
                 nc.vector.tensor_tensor(
-                    g0_first[h][:] if pair == 0 else y_blocks[:, 7 + h : 13 + h : 5, :], bank[:],
-                    g1[:, 2 * pair : 2 * pair + 2, h * HALF : (h + 1) * HALF], ALU.max,
+                    waiting[:, :, half_cols(h)], bank[:], g1[:, 2 * k : 2 * k + 2, half_cols(h)], ALU.max
                 )
 
         woven_y = sb.tile([P, M, PACK], BF16, name="woven_y", align_bytes=64)
         y_codes = sb.tile([P, M], U32, name="y_codes", align_bytes=64)
         y_scales = sb.tile([P, M], U8, name="y_scales", align_bytes=64)
 
-        def scatter(r, first, last, src, on_vector):
-            dst = placed[r][:].indirect(place_list[:, first // 16 : last // 16])
+        def scatter(r, first, last, on_vector):
+            k, e = divmod(BY_PAIR.index(r), 2)
+            src = y[:, PAIRS[k][0], e * J + first : e * J + last]
+            dst = placed[r][:].indirect(entries(place_list, first, last))
             if on_vector:
                 nc.vector.tensor_copy(dst, src)
             else:
@@ -168,44 +185,36 @@ def tile_attend_tab_larger_keep_pl_kernel(
 
         def add_old(r, cols):
             nc.vector.scalar_tensor_tensor(
-                y[:, r, cols], old_rows[r][:, cols], fade_cols[:, r : r + 1], placed[r][:, cols], ALU.mult, ALU.add
+                y[:, r, cols], old_slabs[r][:, cols], fade_cols[:, r : r + 1], placed[r][:, cols], ALU.mult, ALU.add
             )
 
-        def round_rows(cols, on_vector):
-            dst = woven_y[:, cols, :].rearrange("p (c i) r -> p c r i", i=4)
-            src = y[:, :, cols].rearrange("p r (c i) -> p c r i", i=4)
-            if on_vector:
-                nc.vector.tensor_copy(dst, src)
-            else:
-                nc.scalar.copy(dst, src)
-
-        everything = slice(0, M)
-        quarters = [slice(c * M // 4, (c + 1) * M // 4) for c in range(4)]
-        halves = [slice(0, M // 2), slice(M // 2, M)]
-        split = J - 128
-        scatter(3, split, J, y[:, 3, split:J], True)
-        scatter(0, 0, J, y_flat[:, 7 * HALF : 9 * HALF], True)
-        for n in range(2):
+        scatter(LAST, J - LAST_ON_VECTOR, J, True)
+        scatter(OWN, 0, J, True)
+        for r in (FIRST, SECOND):
             for h in range(2):
-                scatter(ORDER[n], h * HALF, (h + 1) * HALF, g0_first[h][:, n, :], False)
-        scatter(3, 0, split, y[:, 3, 0:split], False)
-        for r in (0, 2, 1):
-            add_old(r, everything)
-            nc.sync.dma_start(out_by_slot[r], y[:, r, :])
+                scatter(r, h * HALF, (h + 1) * HALF, False)
+        scatter(LAST, 0, J - LAST_ON_VECTOR, False)
+
+        faded = sb.tile([P, M], F32, name="faded", tag="woven_then_faded", align_bytes=64)
+        nc.gpsimd.tensor_scalar(faded[:], old_slabs[FIRST][:], fade_cols[:, FIRST : FIRST + 1], 0.0, ALU.mult, ALU.add)
+        nc.gpsimd.tensor_tensor(y[:, FIRST, :], faded[:], placed[FIRST][:], ALU.add)
+        nc.sync.dma_start(out_by_slab[FIRST], y[:, FIRST, :])
+        for r in (OWN, SECOND):
+            add_old(r, slice(0, M))
+            nc.sync.dma_start(out_by_slab[r], y[:, r, :])
+
+        quarter0, quarter1, half1 = slice(0, M // 4), slice(M // 4, M // 2), slice(M // 2, M)
         words_out = out_1[0].rearrange("p c r -> p (c r)").bitcast(I32)
-        add_old(PACK - 1, quarters[0])
-        add_old(PACK - 1, slice(M // 4, M))
-        nc.sync.dma_start(out_by_slot[PACK - 1], y[:, PACK - 1, :])
-        for c in range(2):
-            round_rows(quarters[c], False)
-        round_rows(halves[1], True)
-        for c in (1, 0):
-            nc.vector.quantize_mx(
-                y_codes[:, halves[c]].bitcast(FP8X4), y_scales[:, halves[c]],
-                woven_y[:, halves[c], :].rearrange("p m r -> p (m r)"),
-            )
-            nc.sync.dma_start(words_out[:, halves[c]], y_codes[:, halves[c]].bitcast(I32))
-        for q in range(4):
+        for cols in (quarter0, half1, quarter1):
+            add_old(LAST, cols)
+        nc.sync.dma_start(out_by_slab[LAST], y[:, LAST, :])
+        weave(woven_y[:, half1, :], y[:, :, half1], True)
+        for cols in (quarter0, quarter1):
+            weave(woven_y[:, cols, :], y[:, :, cols], False)
+        for cols in (quarter0, half1, quarter1):
+            quantise(y_codes[:, cols], y_scales[:, cols], woven_y[:, cols, :])
+            nc.sync.dma_start(words_out[:, cols], y_codes[:, cols].bitcast(I32))
+        for q in range(QUADRANTS):
             queue = nc.sync if q % 2 == 0 else nc.scalar
             queue.dma_start(
                 out_2[0, 4 * q : 4 * q + 4, :].bitcast(I32), y_scales[32 * q : 32 * q + 4, :].bitcast(I32)

from contextlib import ExitStack

import concourse.mybir as mybir

D, T, I, J, U, M = 512, 2048, 512, 512, 1024, 1024
FLOPS = 2 * 2 * D * I * J

F32 = mybir.dt.float32
BF16 = mybir.dt.bfloat16
I32 = mybir.dt.int32
U32 = mybir.dt.uint32
U16 = mybir.dt.uint16
U8 = mybir.dt.uint8
FP8X4 = mybir.dt.float8_e4m3fn_x4
FP4X4 = mybir.dt.float4_e2m1fn_x4
COPY = mybir.ActivationFunctionType.Copy
ALU = mybir.AluOpType

P = 128
PACK = 4
QUADRANTS = 4
PER_COLUMN = 16
RUN = 4
HALF = J // 2

FIRST, SECOND, OWN, LAST = 0, 1, 2, 3
PAIRS = ((LAST, FIRST), (SECOND, OWN))
BY_PAIR = PAIRS[0] + PAIRS[1]
LAST_ON_VECTOR = 256
WOVEN_ON_SCALAR = 128


def tile_attend_tab_larger_keep_pl_kernel(
    tc, keys_words, keys_scales, notes, users2, old, fade, offs, offs2, offs3, offs4, out_0, out_1, out_2
):
    nc = tc.nc
    with ExitStack() as ctx:
        sb = ctx.enter_context(tc.tile_pool(name="sb", bufs=1))
        ps = ctx.enter_context(tc.psum_pool(name="ps", bufs=1))

        def tiles(name, count, shape, dtype):
            return [sb.tile(shape, dtype, name="%s%d" % (name, n), align_bytes=64) for n in range(count)]

        def entries(offsets, first, last):
            return offsets[:, first // PER_COLUMN : last // PER_COLUMN]

        def half_cols(h):
            return slice(h * HALF, (h + 1) * HALF)

        def gather(dst, slab, offsets, on_vector):
            if on_vector:
                nc.vector.tensor_copy(dst, slab[:].indirect(offsets))
            else:
                nc.scalar.activation(dst, slab[:].indirect(offsets), COPY)

        def weave(dst, src, on_vector):
            dst = dst.rearrange("p (c n) t -> p c t n", n=RUN)
            src = src.rearrange("p t (c n) -> p c t n", n=RUN)
            if on_vector:
                nc.vector.tensor_copy(dst, src)
            else:
                nc.scalar.copy(dst, src)

        def quantise(codes, scales, woven):
            nc.vector.quantize_mx(codes.bitcast(FP8X4), scales, woven.rearrange("p c t -> p (c t)"))

        key_list = sb.tile([P, I // PER_COLUMN], U16, name="key_list")
        note_list = sb.tile([P, J // PER_COLUMN], U16, name="note_list")
        user_list = sb.tile([P, J // PER_COLUMN], U16, name="user_list")
        place_list = sb.tile([P, J // PER_COLUMN], U16, name="place_list")
        key_word_pool = sb.tile([P, T], U16, name="key_word_pool", align_bytes=64)
        key_scale_pool = sb.tile([P, T], U8, name="key_scale_pool", align_bytes=64)
        note_slabs = tiles("note_slab", PACK, [P, U], F32)
        user_slabs = tiles("user_slab", PACK - 1, [P, U], F32)
        user_slabs.append(sb.tile([P, U], F32, name="user_slab_last", tag="last_users_then_g1", align_bytes=64))
        old_slabs = tiles("old_slab", PACK, [P, M], F32)
        placed = tiles("placed", PACK, [P, M], F32)
        fade_cols = sb.tile([P, PACK], F32, name="fade_cols")

        notes_by_slab = notes.rearrange("(p t) u -> t p u", t=PACK)
        users_by_slab = users2.rearrange("(p t) u -> t p u", t=PACK)
        old_by_slab = old.rearrange("(p r) m -> r p m", r=PACK)
        out_by_slab = out_0.rearrange("(p r) m -> r p m", r=PACK)

        nc.vector.memset(key_scale_pool[:].bitcast(I32), 0)
        nc.vector.memset(placed[0][:], 0.0)
        for r in range(1, PACK):
            nc.gpsimd.memset(placed[r][:], 0.0)

        nc.sync.dma_start(note_slabs[0][:], notes_by_slab[0])
        nc.sync.dma_start(note_list[:], offs2)
        nc.sync.dma_start(key_list[:], offs)
        nc.sync.dma_start(key_word_pool[:].bitcast(I32), keys_words[0].bitcast(I32))
        nc.sync.dma_start(user_list[:], offs3)
        nc.sync.dma_start(place_list[:], offs4)
        nc.sync.dma_start(note_slabs[1][:], notes_by_slab[1])
        nc.sync.dma_start(note_slabs[2][:], notes_by_slab[2])
        for q in range(QUADRANTS):
            nc.sync.dma_start(
                key_scale_pool[32 * q : 32 * q + 4, :].bitcast(I32),
                keys_scales[0, 4 * q : 4 * q + 4, :].bitcast(I32),
            )
        nc.sync.dma_start(note_slabs[3][:], notes_by_slab[3])
        for t in range(PACK):
            nc.sync.dma_start(user_slabs[t][:], users_by_slab[t])
        nc.sync.dma_start(fade_cols[:], fade.rearrange("(p r) o -> p (r o)", r=PACK))
        for r in (FIRST, OWN, SECOND, LAST):
            nc.sync.dma_start(old_slabs[r][:], old_by_slab[r])

        picked_words = sb.tile([P, I], U16, name="picked_words", align_bytes=64)
        key_words = sb.tile([P, PACK, P], U16, name="key_words", align_bytes=64)
        key_scales = sb.tile([P, PACK, P], U8, name="key_scales", align_bytes=64)
        nc.vector.tensor_copy(picked_words[:], key_word_pool[:].indirect(key_list[:]))
        nc.vector.tensor_copy(key_scales[:].rearrange("p r s -> p s r"), key_scale_pool[:].indirect(key_list[:]))
        nc.vector.tensor_copy(key_words[:], picked_words[:].rearrange("p (s r) -> p r s", r=PACK))

        def product(bank, r, codes, scales):
            nc.tensor.matmul_mx(
                bank, key_words[:, r, :].bitcast(FP4X4), key_scales[:, r, :], codes.bitcast(FP8X4), scales,
                start=True, stop=True,
            )

        picked_notes = sb.tile([P, PACK, J], BF16, name="picked_notes", align_bytes=64)
        for t in range(PACK):
            if t in (0, PACK - 1):
                gather(picked_notes[:, t, half_cols(0)], note_slabs[t], entries(note_list, 0, HALF), True)
                gather(picked_notes[:, t, half_cols(1)], note_slabs[t], entries(note_list, HALF, J), False)
            else:
                gather(picked_notes[:, t, :], note_slabs[t], note_list[:], False)
        woven_notes = sb.tile([P, J, PACK], BF16, name="woven_notes", align_bytes=64)
        note_codes = sb.tile([P, J], U32, name="note_codes", align_bytes=64)
        note_scales = sb.tile([P, J], U8, name="note_scales", align_bytes=64)
        weave(woven_notes[:], picked_notes[:], True)
        quantise(note_codes[:], note_scales[:], woven_notes[:])
        g1_banks = [ps.tile([P, J], F32, name="g1_bank%d" % r) for r in range(PACK)]
        for r in BY_PAIR:
            product(g1_banks[r][:], r, note_codes[:], note_scales[:])

        picked_users = tiles("picked_users", 2, [P, PACK, HALF], BF16)
        user_codes = tiles("user_codes", 2, [P, HALF], U32)
        user_scales = tiles("user_scales", 2, [P, HALF], U8)
        y = sb.tile([P, PACK, M], F32, name="y", align_bytes=64)
        for t in range(PACK):
            for h in range(2):
                offsets = entries(user_list, h * HALF, (h + 1) * HALF)
                gather(picked_users[h][:, t, :], user_slabs[t], offsets, t >= PACK - 2 and h == 0)
        woven_users = [
            sb.tile([P, HALF, PACK], BF16, name="woven_users0", align_bytes=64),
            sb.tile([P, HALF, PACK], BF16, name="woven_users1", tag="woven_then_faded", align_bytes=64),
        ]
        by_scalar = slice(HALF - WOVEN_ON_SCALAR, HALF)
        weave(woven_users[1][:, by_scalar, :], picked_users[1][:, :, by_scalar], False)

        g1 = sb.tile([P, PACK, J], F32, name="g1", tag="last_users_then_g1", align_bytes=64)
        for n in range(PACK):
            nc.scalar.copy(g1[:, n, :], g1_banks[BY_PAIR[n]][:])

        for h in range(2):
            by_vector = slice(0, HALF if h == 0 else HALF - WOVEN_ON_SCALAR)
            weave(woven_users[h][:, by_vector, :], picked_users[h][:, :, by_vector], True)
            quantise(user_codes[h][:], user_scales[h][:], woven_users[h][:])

        for k, pair in enumerate(PAIRS):
            waiting = y[:, pair[0], :].rearrange("p (e j) -> p e j", e=2)
            for h in range(2):
                bank = ps.tile([P, 2, HALF], F32, name="g2_bank%d%d" % (h, k))
                for e, r in enumerate(pair):
                    product(bank[:, e, :], r, user_codes[h][:], user_scales[h][:])
                nc.vector.tensor_tensor(
                    waiting[:, :, half_cols(h)], bank[:], g1[:, 2 * k : 2 * k + 2, half_cols(h)], ALU.max
                )

        woven_y = sb.tile([P, M, PACK], BF16, name="woven_y", align_bytes=64)
        y_codes = sb.tile([P, M], U32, name="y_codes", align_bytes=64)
        y_scales = sb.tile([P, M], U8, name="y_scales", align_bytes=64)

        def scatter(r, first, last, on_vector):
            k, e = divmod(BY_PAIR.index(r), 2)
            src = y[:, PAIRS[k][0], e * J + first : e * J + last]
            dst = placed[r][:].indirect(entries(place_list, first, last))
            if on_vector:
                nc.vector.tensor_copy(dst, src)
            else:
                nc.scalar.activation(dst, src, COPY)

        def add_old(r, cols):
            nc.vector.scalar_tensor_tensor(
                y[:, r, cols], old_slabs[r][:, cols], fade_cols[:, r : r + 1], placed[r][:, cols], ALU.mult, ALU.add
            )

        scatter(LAST, J - LAST_ON_VECTOR, J, True)
        scatter(OWN, 0, J, True)
        for r in (FIRST, SECOND):
            for h in range(2):
                scatter(r, h * HALF, (h + 1) * HALF, False)
        scatter(LAST, 0, J - LAST_ON_VECTOR, False)

        faded = sb.tile([P, M], F32, name="faded", tag="woven_then_faded", align_bytes=64)
        nc.gpsimd.tensor_scalar(faded[:], old_slabs[FIRST][:], fade_cols[:, FIRST : FIRST + 1], 0.0, ALU.mult, ALU.add)
        nc.gpsimd.tensor_tensor(y[:, FIRST, :], faded[:], placed[FIRST][:], ALU.add)
        nc.sync.dma_start(out_by_slab[FIRST], y[:, FIRST, :])
        for r in (OWN, SECOND):
            add_old(r, slice(0, M))
            nc.sync.dma_start(out_by_slab[r], y[:, r, :])

        quarter0, quarter1, half1 = slice(0, M // 4), slice(M // 4, M // 2), slice(M // 2, M)
        words_out = out_1[0].rearrange("p c r -> p (c r)").bitcast(I32)
        for cols in (quarter0, half1, quarter1):
            add_old(LAST, cols)
        nc.sync.dma_start(out_by_slab[LAST], y[:, LAST, :])
        weave(woven_y[:, half1, :], y[:, :, half1], True)
        for cols in (quarter0, quarter1):
            weave(woven_y[:, cols, :], y[:, :, cols], False)
        for cols in (quarter0, half1, quarter1):
            quantise(y_codes[:, cols], y_scales[:, cols], woven_y[:, cols, :])
            nc.sync.dma_start(words_out[:, cols], y_codes[:, cols].bitcast(I32))
        for q in range(QUADRANTS):
            queue = nc.sync if q % 2 == 0 else nc.scalar
            queue.dma_start(
                out_2[0, 4 * q : 4 * q + 4, :].bitcast(I32), y_scales[32 * q : 32 * q + 4, :].bitcast(I32)
            )
